import numpy as np
import ml_dtypes


def mxq(x, axis, fmt="e4m3"):
    dtype, down = {"e4m3": (ml_dtypes.float8_e4m3fn, 7), "e5m2": (ml_dtypes.float8_e5m2, 14)}[fmt]
    v = np.moveaxis(np.asarray(x, np.float32).astype(ml_dtypes.bfloat16).astype(np.float64), axis, -1)
    blocks = v.reshape(v.shape[:-1] + (-1, 32))
    amax = np.abs(blocks).max(-1, keepdims=True)
    byte = np.maximum(np.where(amax > 0, np.frexp(amax)[1] - 1 + 127, 0) - down, 1)
    scale = np.exp2(byte - 127.0)
    codes = (blocks / scale).astype(np.float32).astype(dtype).astype(np.float64)
    return np.moveaxis((codes * scale).reshape(v.shape), -1, axis)


WIDE = False


def mx_kscale(k):
    if not WIDE:
        return np.ones(k)
    levels = np.array([10, -10, 5, -5, 0])
    if k % 512:
        return np.exp2(np.random.permutation(np.resize(levels, k // 32))).repeat(32)
    a = np.empty((k // 512, 16))
    for p in range(k // 512):
        a[p, :8] = np.random.permutation(np.resize(levels, 8))
        for g in range(8):
            far = levels[np.abs(levels - a[p, g]) >= 10]
            a[p, g + 8] = far[np.random.randint(len(far))]
    return np.exp2(a.ravel()).repeat(32)


def f64(x):
    return np.asarray(x).astype(np.float64)


def striped(idx):
    return np.tile(np.asarray(idx).reshape(-1, 16).T, (8, 1)).astype(np.uint16)


def unstriped(offs):
    return offs[:16].T.reshape(-1).astype(np.int64)


def striped8(idx):
    return np.asarray(idx).reshape(8, -1, 16).transpose(0, 2, 1).reshape(128, -1).astype(np.uint16)


def unstriped8(offs):
    return offs.reshape(8, 16, -1).transpose(0, 2, 1).reshape(8, -1).astype(np.int64)


def pick8(x, idx, run):
    r = np.arange(len(x))
    return x[r[:, None], idx[r % (8 * run) // run]]


E2M1 = np.array([0.0, 0.5, 1.0, 1.5, 2.0, 3.0, 4.0, 6.0, -0.0, -0.5, -1.0, -1.5, -2.0, -3.0, -4.0, -6.0])


def pack_weight(w, fmt):
    k, n = w.shape
    w = f64(np.asarray(w, np.float32).astype(ml_dtypes.bfloat16)).reshape(k // 32, 32, n)
    amax = np.abs(w).max(1)
    if fmt == "e4m3":
        byte = np.frexp(amax)[1] - 1 + 127 - 7
    else:
        mant, ex = np.frexp(amax / 6.0)
        byte = np.where(mant > 0.5, ex, ex - 1) + 127
    byte = np.clip(np.where(amax > 0, byte, 1), 1, 254)
    scaled = (w * np.exp2(127.0 - byte)[:, None, :]).reshape(k, n).astype(np.float32)
    by_word = np.ascontiguousarray(scaled.reshape(k // 512, 128, 4, n).transpose(0, 1, 3, 2))
    if fmt == "e4m3":
        words = by_word.astype(ml_dtypes.float8_e4m3fn).view(np.uint8)
    else:
        c = by_word.astype(ml_dtypes.float4_e2m1fn).view(np.uint8) & 0xF
        words = (c[..., 0::2] | (c[..., 1::2] << 4)).reshape(k // 512, 128, 2 * n)
    return np.ascontiguousarray(words), np.ascontiguousarray(byte.astype(np.uint8).reshape(k // 512, 16, n))


def unpack_weight(words, scales, fmt):
    g, _, n = scales.shape
    words = np.ascontiguousarray(words).reshape(g, 128, n, -1)
    if fmt == "e4m3":
        vals = words.view(ml_dtypes.float8_e4m3fn).astype(np.float64)
    else:
        nib = np.empty((g, 128, n, 4), np.uint8)
        nib[..., 0::2] = words & 0xF
        nib[..., 1::2] = words >> 4
        vals = E2M1[nib]
    vals = vals * np.repeat(np.exp2(scales.astype(np.float64) - 127.0), 8, axis=1)[..., None]
    return vals.transpose(0, 1, 3, 2).reshape(g * 512, n)


K, J, R, T, Z, M, O, N, U, E, G = 512, 512, 512, 2048, 512, 1024, 256, 256, 512, 128, 256


def setup_inputs():
    n = np.random.standard_normal
    idx = np.random.permutation(T)[:J]
    idx2 = np.random.permutation(M)[:J]
    idx3 = np.stack([np.random.permutation(J)[:O] for _ in range(8)])
    idx4 = np.stack([np.random.permutation(U)[:O] for _ in range(8)])
    idx5 = np.stack([np.random.permutation(O)[:E] for _ in range(8)])
    idx6 = np.stack([np.random.permutation(G)[:E] for _ in range(8)])
    fk = mx_kscale(K)
    fr = mx_kscale(R)
    fz = mx_kscale(Z)
    xtp = pack_weight(n((K, T)) * fk[:, None], "e4m3")
    wp = pack_weight(n((K, R)) * 1 / np.sqrt(K) / fk[:, None] * fr, "e4m3")
    xop = pack_weight(n((Z, M)) / fz[:, None], "e4m3")
    w2p = pack_weight(n((Z, R)) * 1 / np.sqrt(Z) * fz[:, None] * fr, "e2m1")
    wbp = pack_weight(n((R, N)) * 1 / np.sqrt(R) / fr[:, None], "e2m1")
    wop = pack_weight(n((R, N)) * 1 / np.sqrt(R) / fr[:, None], "e4m3")
    return {
        "xt_words": xtp[0],
        "xt_scales": xtp[1],
        "w_words": wp[0],
        "w_scales": wp[1],
        "xo_words": xop[0],
        "xo_scales": xop[1],
        "w2_words": w2p[0],
        "w2_scales": w2p[1],
        "sa": (np.random.uniform(0.5, 1.6, (R, 1))).astype(np.float32),
        "wb_words": wbp[0],
        "wb_scales": wbp[1],
        "wo_words": wop[0],
        "wo_scales": wop[1],
        "se": (np.random.uniform(0.5, 1.6, (N, 1))).astype(np.float32),
        "offs": striped(idx),
        "offs2": striped(idx2),
        "offs3": striped8(idx3),
        "offs4": striped8(idx4),
        "offs5": striped8(idx5),
        "offs6": striped8(idx6),
    }


def reference(xt_words, xt_scales, w_words, w_scales, xo_words, xo_scales, w2_words, w2_scales, sa, wb_words, wb_scales, wo_words, wo_scales, se, offs, offs2, offs3, offs4, offs5, offs6):
    idx = unstriped(offs)
    idx2 = unstriped(offs2)
    idx3 = unstriped8(offs3)
    idx4 = unstriped8(offs4)
    idx5 = unstriped8(offs5)
    idx6 = unstriped8(offs6)
    xtu = unpack_weight(xt_words, xt_scales, "e4m3")
    wu = unpack_weight(w_words, w_scales, "e4m3")
    xou = unpack_weight(xo_words, xo_scales, "e4m3")
    w2u = unpack_weight(w2_words, w2_scales, "e2m1")
    wbu = unpack_weight(wb_words, wb_scales, "e2m1")
    wou = unpack_weight(wo_words, wo_scales, "e4m3")
    xtidxg = xtu[:, idx]
    xoidx2g = xou[:, idx2]
    a = wu.T @ xtidxg + w2u.T @ xoidx2g
    g1 = np.maximum(a, 0.0)
    hid = pick8(g1, idx3, 64) * f64(sa)
    hidq = mxq(hid, 0, "e4m3")
    p = wbu.T @ hidq
    q = wou.T @ hidq
    m0 = np.zeros((N, U))
    m0[np.arange(N)[:, None], idx4[np.arange(N) % 128 // 16]] = p
    m1 = pick8(q, idx5, 16) * f64(se)
    m2 = np.zeros((N, G))
    m2[np.arange(N)[:, None], idx6[np.arange(N) % 128 // 16]] = m1
    m3 = np.repeat(m2, U // G, axis=1)
    y = m0 - m3
    return y

@@ -1,0 +1,232 @@
+from contextlib import ExitStack
+
+import concourse.mybir as mybir
+
+K, J, R, T, Z, M, O, N, U, E, G = 512, 512, 512, 2048, 512, 1024, 256, 256, 512, 128, 256
+FLOPS = 2 * (K * R * J + Z * R * J + 2 * R * N * O)
+
+F32 = mybir.dt.float32
+BF16 = mybir.dt.bfloat16
+I32 = mybir.dt.int32
+U32 = mybir.dt.uint32
+U16 = mybir.dt.uint16
+U8 = mybir.dt.uint8
+FP8X4 = mybir.dt.float8_e4m3fn_x4
+FP4X4 = mybir.dt.float4_e2m1fn_x4
+ACT = mybir.ActivationFunctionType
+ALU = mybir.AluOpType
+
+P = 128
+PACK = 4
+QUADS = 4
+JH = J // 2
+OH = O // 2
+XT_ROW = 4
+W_ROW = 8
+WO_ROW = 12
+
+
+def tile_picked_tokens_plain_bank_kept_outcomes_endcoarse_kernel(
+    tc, xt_words, xt_scales, w_words, w_scales, xo_words, xo_scales, w2_words, w2_scales, sa,
+    wb_words, wb_scales, wo_words, wo_scales, se, offs, offs2, offs3, offs4, offs5, offs6, out
+):
+    nc = tc.nc
+    with ExitStack() as ctx:
+        sb = ctx.enter_context(tc.tile_pool(name="sb", bufs=1))
+        ps = ctx.enter_context(tc.psum_pool(name="ps", bufs=1))
+
+        def tile(name, shape, dtype):
+            return sb.tile(shape, dtype, name=name, align_bytes=64)
+
+        def load_list(name, src):
+            t = tile(name, list(src.shape), U16)
+            nc.sync.dma_start(out=t[:], in_=src)
+            return t
+
+        def load_words(eng, name, src, cols):
+            t = tile(name, [P, cols], U32)
+            eng.dma_start(out=t[:].bitcast(I32), in_=src[0].rearrange("p n t -> p (n t)").bitcast(I32))
+            return t
+
+        def load_nibbles(eng, name, src, cols):
+            t = tile(name, [P, 2 * cols], U8)
+            eng.dma_start(out=t[:].bitcast(I32), in_=src[0].bitcast(I32))
+            return t
+
+        def zeroed(name, cols):
+            t = tile(name, [P, cols], U8)
+            nc.vector.memset(t[:].bitcast(I32), 0)
+            return t
+
+        def load_rows(eng, plane, src, row, q):
+            eng.dma_start(
+                out=plane[32 * q + row : 32 * q + row + 4, :].bitcast(I32),
+                in_=src[0, 4 * q : 4 * q + 4, :].bitcast(I32),
+            )
+
+        def load_stage(eng, stage, src, row):
+            eng.dma_start(
+                out=stage[row : row + 4, :].bitcast(I32).rearrange("r (q c) -> r q c", q=QUADS),
+                in_=src[0].bitcast(I32).rearrange("(q r) c -> r q c", r=4),
+            )
+
+        def spread(stage, cols):
+            for q in range(1, QUADS):
+                nc.vector.tensor_copy(
+                    stage[32 * q : 32 * (q + 1), :cols].bitcast(I32), stage[:32, cols * q : cols * (q + 1)].bitcast(I32)
+                )
+
+        xo_s = zeroed("xo_s", M)
+        ww_s = zeroed("ww_s", QUADS * R)
+        xt_s = zeroed("xt_s", T)
+        wbo_s = zeroed("wbo_s", QUADS * N)
+        m0 = [tile(f"m0_{i}", [P, U], F32) for i in range(2)]
+        m2 = [tile(f"m2_{i}", [P, G], F32) for i in range(2)]
+        for i in range(2):
+            nc.vector.memset(m0[i][:], 0.0)
+            nc.vector.memset(m2[i][:], 0.0)
+
+        l2 = load_list("l2", offs2)
+        xo_w = load_words(nc.scalar, "xo_w", xo_words, M)
+        w2_w = load_nibbles(nc.gpsimd, "w2_w", w2_words, R)
+        w_w = load_words(nc.gpsimd, "w_w", w_words, R)
+        for q in range(QUADS):
+            load_rows(nc.sync, xo_s, xo_scales, 0, q)
+        load_stage(nc.sync, ww_s, w2_scales, 0)
+        load_stage(nc.sync, ww_s, w_scales, W_ROW)
+        l1 = load_list("l1", offs)
+        for q in range(QUADS):
+            load_rows(nc.sync, xt_s, xt_scales, XT_ROW, q)
+        xt_w = load_words(nc.sync, "xt_w", xt_words, T)
+        l3 = load_list("l3", offs3)
+        sa_t = tile("sa_t", [P, PACK], F32)
+        nc.sync.dma_start(out=sa_t[:], in_=sa.rearrange("(p t) o -> p (t o)", t=PACK))
+        load_stage(nc.sync, wbo_s, wb_scales, 0)
+        load_stage(nc.sync, wbo_s, wo_scales, WO_ROW)
+        wb_w = load_nibbles(nc.sync, "wb_w", wb_words, N)
+        wo_w = load_words(nc.sync, "wo_w", wo_words, N)
+        l4 = load_list("l4", offs4)
+        l5 = load_list("l5", offs5)
+        l6 = load_list("l6", offs6)
+        se_t = tile("se_t", [P, 2], F32)
+        with nc.allow_non_contiguous_dma(reason="one weight a partition"):
+            nc.sync.dma_start(out=se_t[:], in_=se.rearrange("(i p) o -> p (i o)", p=P))
+
+        xo_sg = tile("xo_sg", [P, J], U8)
+        nc.vector.tensor_copy(xo_sg[:], xo_s[:].indirect(l2[:]))
+        spread(ww_s, R)
+        xo_wg = tile("xo_wg", [P, J], U32)
+        nc.vector.tensor_copy(xo_wg[:], xo_w[:].indirect(l2[:]))
+
+        w2_d = tile("w2_d", [P, 2 * R], U8)
+        nc.scalar.copy(
+            out=w2_d[:].bitcast(U16).rearrange("p (t m) -> p m t", t=PACK),
+            in_=w2_w[:].bitcast(U16).rearrange("p (m t) -> p m t", t=PACK),
+        )
+        ww_sd = tile("ww_sd", [P, R], U8)
+        nc.gpsimd.tensor_copy(
+            out=ww_sd[:].rearrange("p (t m) -> p t m", t=PACK),
+            in_=ww_s[:, :R].rearrange("p (m t) -> p t m", t=PACK),
+        )
+        banks = [[ps.tile([P, JH], F32, name=f"a{t}{jh}", tag=f"bank{2 * t + jh}") for jh in range(2)] for t in range(PACK)]
+        for jh in range(2):
+            for t in range(PACK):
+                nc.tensor.matmul_mx(
+                    banks[t][jh][:],
+                    lhsT=w2_d[:, 2 * P * t : 2 * P * (t + 1)].bitcast(FP4X4),
+                    lhsT_scale=ww_sd[:, P * t : P * (t + 1)],
+                    rhs=xo_wg[:, JH * jh : JH * (jh + 1)].bitcast(FP8X4),
+                    rhs_scale=xo_sg[:, JH * jh : JH * (jh + 1)],
+                    start=True,
+                    stop=False,
+                )
+
+        xt_sg = tile("xt_sg", [P, J], U8)
+        nc.vector.tensor_copy(xt_sg[:], xt_s[:].indirect(l1[:]))
+        w_d = tile("w_d", [P, R], U32)
+        nc.scalar.copy(
+            out=w_d[:].rearrange("p (t m) -> p m t", t=PACK),
+            in_=w_w[:].rearrange("p (m t) -> p m t", t=PACK),
+        )
+        g1 = [tile(f"g1_{t}", [P, J], F32) for t in range(PACK)]
+        for jh in range(2):
+            xt_wg = tile(f"xt_wg{jh}", [P, JH], U32)
+            nc.vector.tensor_copy(xt_wg[:], xt_w[:].indirect(l1[:, JH // 16 * jh : JH // 16 * (jh + 1)]))
+            for t in range(PACK):
+                nc.tensor.matmul_mx(
+                    banks[t][jh][:],
+                    lhsT=w_d[:, P * t : P * (t + 1)].bitcast(FP8X4),
+                    lhsT_scale=ww_sd[W_ROW:, P * t : P * (t + 1)],
+                    rhs=xt_wg[:].bitcast(FP8X4),
+                    rhs_scale=xt_sg[XT_ROW:, JH * jh : JH * (jh + 1)],
+                    start=False,
+                    stop=True,
+                )
+        spread(wbo_s, N)
+        for t in range(PACK):
+            nc.scalar.activation(out=g1[t][:, :JH], in_=banks[t][0][:], func=ACT.Relu)
+        for t in range(PACK):
+            nc.vector.tensor_scalar_max(g1[t][:, JH:], banks[t][1][:], 0.0)
+
+        planes = [tile(f"planes{h}", [P, PACK, OH], BF16) for h in range(2)]
+        for h in range(2):
+            for t in range(PACK):
+                nc.scalar.activation(
+                    out=planes[h][:, t, :],
+                    in_=g1[t][:].indirect(l3[:, OH // 16 * h : OH // 16 * (h + 1)]),
+                    func=ACT.Copy,
+                    scale=sa_t[:, t : t + 1],
+                )
+
+        p_sb = [[tile(f"p_sb{i}{h}", [P, OH], F32) for h in range(2)] for i in range(2)]
+        q_sb = [tile(f"q_sb{i}", [P, O], F32) for i in range(2)]
+        for h in range(2):
+            woven = tile("woven", [P, OH, PACK], BF16)
+            nc.vector.tensor_copy(woven[:], planes[h][:].rearrange("p t n -> p n t"))
+            codes = tile(f"codes{h}", [P, OH], U32)
+            scales = tile(f"scales{h}", [P, OH], U8)
+            nc.vector.quantize_mx(codes[:].bitcast(FP8X4), scales[:], woven[:].rearrange("p n t -> p (n t)"))
+            for which in ((0, 1) if h == 0 else (1, 0)):
+                for i in range(2):
+                    acc = ps.tile([P, OH], F32, name=f"acc{h}{which}{i}", tag=f"bank{2 * (2 * which + i) + h}")
+                    if which == 0:
+                        lhsT = wb_w[:, 2 * P * i : 2 * P * (i + 1)].bitcast(FP4X4)
+                        lhsT_scale = wbo_s[:, P * i : P * (i + 1)]
+                        dst = p_sb[i][h][:]
+                    else:
+                        lhsT = wo_w[:, P * i : P * (i + 1)].bitcast(FP8X4)
+                        lhsT_scale = wbo_s[WO_ROW:, P * i : P * (i + 1)]
+                        dst = q_sb[i][:, OH * h : OH * (h + 1)]
+                    nc.tensor.matmul_mx(
+                        acc[:], lhsT=lhsT, lhsT_scale=lhsT_scale, rhs=codes[:].bitcast(FP8X4), rhs_scale=scales[:],
+                        start=True, stop=True,
+                    )
+                    if (h, which, i) == (0, 0, 0):
+                        nc.scalar.copy(dst, acc[:])
+                    else:
+                        nc.vector.tensor_copy(dst, acc[:])
+
+        def put_p(i, h):
+            nc.scalar.activation(
+                out=m0[i][:].indirect(l4[:, OH // 16 * h : OH // 16 * (h + 1)]), in_=p_sb[i][h][:], func=ACT.Copy
+            )
+
+        for i in range(2):
+            put_p(i, 0)
+        m1 = [tile(f"m1_{i}", [P, E], F32) for i in range(2)]
+        for i in range(2):
+            nc.scalar.activation(out=m1[i][:], in_=q_sb[i][:].indirect(l5[:]), func=ACT.Copy, scale=se_t[:, i : i + 1])
+        for i in range(2):
+            nc.scalar.activation(out=m2[i][:].indirect(l6[:]), in_=m1[i][:], func=ACT.Copy)
+            put_p(i, 1)
+            for c in range(2):
+                y = tile(f"y{i}{c}", [P, G // 2, 2], F32)
+                nc.vector.tensor_tensor(
+                    y[:],
+                    m0[i][:, U // 2 * c : U // 2 * (c + 1)].rearrange("p (g d) -> p g d", d=2),
+                    m2[i][:, G // 2 * c : G // 2 * (c + 1)].unsqueeze(2).to_broadcast([P, G // 2, 2]),
+                    ALU.subtract,
+                )
+                nc.sync.dma_start(
+                    out=out[P * i : P * (i + 1), U // 2 * c : U // 2 * (c + 1)], in_=y[:].rearrange("p g d -> p (g d)")
+                )

@@ -22,7 +22,7 @@ QUADS = 4
 JH = J // 2
 OH = O // 2
 XT_ROW = 4
-W_ROW = 8
+W_ROW = 4
 WO_ROW = 12
 
 
@@ -35,8 +35,8 @@ def tile_picked_tokens_plain_bank_kept_outcomes_endcoarse_kernel(
         sb = ctx.enter_context(tc.tile_pool(name="sb", bufs=1))
         ps = ctx.enter_context(tc.psum_pool(name="ps", bufs=1))
 
-        def tile(name, shape, dtype):
-            return sb.tile(shape, dtype, name=name, align_bytes=64)
+        def tile(name, shape, dtype, tag=None):
+            return sb.tile(shape, dtype, name=name, tag=tag or name, align_bytes=64)
 
         def load_list(name, src):
             t = tile(name, list(src.shape), U16)
@@ -70,30 +70,33 @@ def tile_picked_tokens_plain_bank_kept_outcomes_endcoarse_kernel(
                 in_=src[0].bitcast(I32).rearrange("(q r) c -> r q c", r=4),
             )
 
-        def spread(stage, cols):
-            for q in range(1, QUADS):
+        def spread(plane, stage, cols, quads):
+            for q in quads:
                 nc.vector.tensor_copy(
-                    stage[32 * q : 32 * (q + 1), :cols].bitcast(I32), stage[:32, cols * q : cols * (q + 1)].bitcast(I32)
+                    plane[32 * q : 32 * (q + 1), :cols].bitcast(I32), stage[:32, cols * q : cols * (q + 1)].bitcast(I32)
                 )
 
         xo_s = zeroed("xo_s", M)
-        ww_s = zeroed("ww_s", QUADS * R)
         xt_s = zeroed("xt_s", T)
+        ww_s = zeroed("ww_s", 2 * R)
+        ww_stage = tile("ww_stage", [8, QUADS * R], U8)
         wbo_s = zeroed("wbo_s", QUADS * N)
+        floor = tile("floor", [P, 1], F32)
+        nc.vector.memset(floor[:], 0.0)
         m0 = [tile(f"m0_{i}", [P, U], F32) for i in range(2)]
         m2 = [tile(f"m2_{i}", [P, G], F32) for i in range(2)]
-        for i in range(2):
-            nc.vector.memset(m0[i][:], 0.0)
-            nc.vector.memset(m2[i][:], 0.0)
 
         l2 = load_list("l2", offs2)
-        xo_w = load_words(nc.scalar, "xo_w", xo_words, M)
-        w2_w = load_nibbles(nc.gpsimd, "w2_w", w2_words, R)
         w_w = load_words(nc.gpsimd, "w_w", w_words, R)
+        for i in range(2):
+            nc.gpsimd.memset(m0[i][:], 0.0)
+            nc.gpsimd.memset(m2[i][:], 0.0)
+        load_stage(nc.sync, ww_stage, w2_scales, 0)
+        load_stage(nc.sync, ww_stage, w_scales, W_ROW)
         for q in range(QUADS):
             load_rows(nc.sync, xo_s, xo_scales, 0, q)
-        load_stage(nc.sync, ww_s, w2_scales, 0)
-        load_stage(nc.sync, ww_s, w_scales, W_ROW)
+        xo_w = load_words(nc.sync, "xo_w", xo_words, M)
+        w2_w = load_nibbles(nc.sync, "w2_w", w2_words, R)
         l1 = load_list("l1", offs)
         for q in range(QUADS):
             load_rows(nc.sync, xt_s, xt_scales, XT_ROW, q)
@@ -112,30 +115,35 @@ def tile_picked_tokens_plain_bank_kept_outcomes_endcoarse_kernel(
         with nc.allow_non_contiguous_dma(reason="one weight a partition"):
             nc.sync.dma_start(out=se_t[:], in_=se.rearrange("(i p) o -> p (i o)", p=P))
 
+        stage_i = ww_stage[:].bitcast(I32).rearrange("r (a b c) -> r a b c", a=2, b=2)
+        plane_i = ww_s[:].bitcast(I32).rearrange("p (a c) -> p a c", a=2)
+        nc.vector.tensor_copy(plane_i[0:8], stage_i[:, :, 0, :])
+        for a in range(2):
+            nc.vector.tensor_copy(plane_i[32:40, a, :], stage_i[:, a, 1, :])
+        nc.vector.tensor_copy(plane_i[64:128, 0, :], plane_i[0:64, 1, :])
+        ww_sd = tile("ww_sd", [P, R], U8)
+        nc.vector.tensor_copy(
+            out=ww_sd[:].rearrange("p (t m) -> p t m", t=PACK),
+            in_=ww_s[:, :R].rearrange("p (m t) -> p t m", t=PACK),
+        )
         xo_sg = tile("xo_sg", [P, J], U8)
         nc.vector.tensor_copy(xo_sg[:], xo_s[:].indirect(l2[:]))
-        spread(ww_s, R)
-        xo_wg = tile("xo_wg", [P, J], U32)
-        nc.vector.tensor_copy(xo_wg[:], xo_w[:].indirect(l2[:]))
 
         w2_d = tile("w2_d", [P, 2 * R], U8)
         nc.scalar.copy(
             out=w2_d[:].bitcast(U16).rearrange("p (t m) -> p m t", t=PACK),
             in_=w2_w[:].bitcast(U16).rearrange("p (m t) -> p m t", t=PACK),
         )
-        ww_sd = tile("ww_sd", [P, R], U8)
-        nc.gpsimd.tensor_copy(
-            out=ww_sd[:].rearrange("p (t m) -> p t m", t=PACK),
-            in_=ww_s[:, :R].rearrange("p (m t) -> p t m", t=PACK),
-        )
         banks = [[ps.tile([P, JH], F32, name=f"a{t}{jh}", tag=f"bank{2 * t + jh}") for jh in range(2)] for t in range(PACK)]
         for jh in range(2):
+            xo_wg = tile(f"xo_wg{jh}", [P, JH], U32)
+            nc.vector.tensor_copy(xo_wg[:], xo_w[:].indirect(l2[:, JH // 16 * jh : JH // 16 * (jh + 1)]))
             for t in range(PACK):
                 nc.tensor.matmul_mx(
                     banks[t][jh][:],
                     lhsT=w2_d[:, 2 * P * t : 2 * P * (t + 1)].bitcast(FP4X4),
                     lhsT_scale=ww_sd[:, P * t : P * (t + 1)],
-                    rhs=xo_wg[:, JH * jh : JH * (jh + 1)].bitcast(FP8X4),
+                    rhs=xo_wg[:].bitcast(FP8X4),
                     rhs_scale=xo_sg[:, JH * jh : JH * (jh + 1)],
                     start=True,
                     stop=False,
@@ -162,13 +170,15 @@ def tile_picked_tokens_plain_bank_kept_outcomes_endcoarse_kernel(
                     start=False,
                     stop=True,
                 )
-        spread(wbo_s, N)
-        for t in range(PACK):
+        for t in range(PACK - 1):
             nc.scalar.activation(out=g1[t][:, :JH], in_=banks[t][0][:], func=ACT.Relu)
+        nc.vector.tensor_scalar_max(g1[PACK - 1][:, :JH], banks[PACK - 1][0][:], floor[:])
         for t in range(PACK):
-            nc.vector.tensor_scalar_max(g1[t][:, JH:], banks[t][1][:], 0.0)
+            nc.vector.tensor_scalar_max(g1[t][:, JH:], banks[t][1][:], floor[:])
+        wbo_p = tile("wbo_p", [P, N], U8, tag="floor")
+        spread(wbo_p, wbo_s, N, range(QUADS))
 
-        planes = [tile(f"planes{h}", [P, PACK, OH], BF16) for h in range(2)]
+        planes = [tile("planes0", [P, PACK, OH], BF16), tile("planes1", [P, PACK, OH], BF16, tag="wbo_s")]
         for h in range(2):
             for t in range(PACK):
                 nc.scalar.activation(
@@ -191,17 +201,17 @@ def tile_picked_tokens_plain_bank_kept_outcomes_endcoarse_kernel(
                     acc = ps.tile([P, OH], F32, name=f"acc{h}{which}{i}", tag=f"bank{2 * (2 * which + i) + h}")
                     if which == 0:
                         lhsT = wb_w[:, 2 * P * i : 2 * P * (i + 1)].bitcast(FP4X4)
-                        lhsT_scale = wbo_s[:, P * i : P * (i + 1)]
+                        lhsT_scale = wbo_p[:, P * i : P * (i + 1)]
                         dst = p_sb[i][h][:]
                     else:
                         lhsT = wo_w[:, P * i : P * (i + 1)].bitcast(FP8X4)
-                        lhsT_scale = wbo_s[WO_ROW:, P * i : P * (i + 1)]
+                        lhsT_scale = wbo_p[WO_ROW:, P * i : P * (i + 1)]
                         dst = q_sb[i][:, OH * h : OH * (h + 1)]
                     nc.tensor.matmul_mx(
                         acc[:], lhsT=lhsT, lhsT_scale=lhsT_scale, rhs=codes[:].bitcast(FP8X4), rhs_scale=scales[:],
                         start=True, stop=True,
                     )
-                    if (h, which, i) == (0, 0, 0):
+                    if (h, which) == (0, 0):
                         nc.scalar.copy(dst, acc[:])
                     else:
                         nc.vector.tensor_copy(dst, acc[:])

@@ -84,13 +84,10 @@ def tile_picked_tokens_plain_bank_kept_outcomes_endcoarse_kernel(
         floor = tile("floor", [P, 1], F32)
         nc.vector.memset(floor[:], 0.0)
         m0 = [tile(f"m0_{i}", [P, U], F32) for i in range(2)]
-        m2 = [tile(f"m2_{i}", [P, G], F32) for i in range(2)]
+        for i in range(2):
+            nc.vector.memset(m0[i][:], 0.0)
 
         l2 = load_list("l2", offs2)
-        w_w = load_words(nc.gpsimd, "w_w", w_words, R)
-        for i in range(2):
-            nc.gpsimd.memset(m0[i][:], 0.0)
-            nc.gpsimd.memset(m2[i][:], 0.0)
         load_stage(nc.sync, ww_stage, w2_scales, 0)
         load_stage(nc.sync, ww_stage, w_scales, W_ROW)
         for q in range(QUADS):
@@ -101,6 +98,7 @@ def tile_picked_tokens_plain_bank_kept_outcomes_endcoarse_kernel(
         for q in range(QUADS):
             load_rows(nc.sync, xt_s, xt_scales, XT_ROW, q)
         xt_w = load_words(nc.sync, "xt_w", xt_words, T)
+        w_w = load_words(nc.sync, "w_w", w_words, R)
         l3 = load_list("l3", offs3)
         sa_t = tile("sa_t", [P, PACK], F32)
         nc.sync.dma_start(out=sa_t[:], in_=sa.rearrange("(p t) o -> p (t o)", t=PACK))
@@ -131,8 +129,8 @@ def tile_picked_tokens_plain_bank_kept_outcomes_endcoarse_kernel(
 
         w2_d = tile("w2_d", [P, 2 * R], U8)
         nc.scalar.copy(
-            out=w2_d[:].bitcast(U16).rearrange("p (t m) -> p m t", t=PACK),
-            in_=w2_w[:].bitcast(U16).rearrange("p (m t) -> p m t", t=PACK),
+            out=w2_d[:].bitcast(U16).rearrange("p (t c i) -> p c t i", t=PACK, i=8),
+            in_=w2_w[:].bitcast(U16).rearrange("p (c i t) -> p c t i", t=PACK, i=8),
         )
         banks = [[ps.tile([P, JH], F32, name=f"a{t}{jh}", tag=f"bank{2 * t + jh}") for jh in range(2)] for t in range(PACK)]
         for jh in range(2):
@@ -152,10 +150,8 @@ def tile_picked_tokens_plain_bank_kept_outcomes_endcoarse_kernel(
         xt_sg = tile("xt_sg", [P, J], U8)
         nc.vector.tensor_copy(xt_sg[:], xt_s[:].indirect(l1[:]))
         w_d = tile("w_d", [P, R], U32)
-        nc.scalar.copy(
-            out=w_d[:].rearrange("p (t m) -> p m t", t=PACK),
-            in_=w_w[:].rearrange("p (m t) -> p m t", t=PACK),
-        )
+        for t in range(PACK):
+            nc.scalar.copy(out=w_d[:, P * t : P * (t + 1)], in_=w_w[:, t::PACK])
         g1 = [tile(f"g1_{t}", [P, J], F32) for t in range(PACK)]
         for jh in range(2):
             xt_wg = tile(f"xt_wg{jh}", [P, JH], U32)
@@ -189,10 +185,15 @@ def tile_picked_tokens_plain_bank_kept_outcomes_endcoarse_kernel(
                 )
 
         p_sb = [[tile(f"p_sb{i}{h}", [P, OH], F32) for h in range(2)] for i in range(2)]
+        m2 = []
         q_sb = [tile(f"q_sb{i}", [P, O], F32) for i in range(2)]
         for h in range(2):
             woven = tile("woven", [P, OH, PACK], BF16)
-            nc.vector.tensor_copy(woven[:], planes[h][:].rearrange("p t n -> p n t"))
+            nc.vector.tensor_copy(
+                woven[:].rearrange("p (c i) t -> p c t i", i=4), planes[h][:].rearrange("p t (c i) -> p c t i", i=4)
+            )
+            m2.append(tile(f"m2_{h}", [P, G], F32, tag=("planes0", "wbo_s")[h]))
+            nc.vector.memset(m2[h][:], 0.0)
             codes = tile(f"codes{h}", [P, OH], U32)
             scales = tile(f"scales{h}", [P, OH], U8)
             nc.vector.quantize_mx(codes[:].bitcast(FP8X4), scales[:], woven[:].rearrange("p n t -> p (n t)"))
@@ -237,6 +238,6 @@ def tile_picked_tokens_plain_bank_kept_outcomes_endcoarse_kernel(
                     m2[i][:, G // 2 * c : G // 2 * (c + 1)].unsqueeze(2).to_broadcast([P, G // 2, 2]),
                     ALU.subtract,
                 )
-                nc.sync.dma_start(
+                (nc.scalar if (i, c) == (1, 1) else nc.sync).dma_start(
                     out=out[P * i : P * (i + 1), U // 2 * c : U // 2 * (c + 1)], in_=y[:].rearrange("p g d -> p (g d)")
                 )

@@ -87,13 +87,13 @@ def tile_picked_tokens_plain_bank_kept_outcomes_endcoarse_kernel(
         for i in range(2):
             nc.vector.memset(m0[i][:], 0.0)
 
-        l2 = load_list("l2", offs2)
+        w2_w = load_nibbles(nc.gpsimd, "w2_w", w2_words, R)
         load_stage(nc.sync, ww_stage, w2_scales, 0)
         load_stage(nc.sync, ww_stage, w_scales, W_ROW)
+        l2 = load_list("l2", offs2)
         for q in range(QUADS):
             load_rows(nc.sync, xo_s, xo_scales, 0, q)
         xo_w = load_words(nc.sync, "xo_w", xo_words, M)
-        w2_w = load_nibbles(nc.sync, "w2_w", w2_words, R)
         l1 = load_list("l1", offs)
         for q in range(QUADS):
             load_rows(nc.sync, xt_s, xt_scales, XT_ROW, q)
@@ -120,7 +120,7 @@ def tile_picked_tokens_plain_bank_kept_outcomes_endcoarse_kernel(
             nc.vector.tensor_copy(plane_i[32:40, a, :], stage_i[:, a, 1, :])
         nc.vector.tensor_copy(plane_i[64:128, 0, :], plane_i[0:64, 1, :])
         ww_sd = tile("ww_sd", [P, R], U8)
-        nc.vector.tensor_copy(
+        nc.gpsimd.tensor_copy(
             out=ww_sd[:].rearrange("p (t m) -> p t m", t=PACK),
             in_=ww_s[:, :R].rearrange("p (m t) -> p t m", t=PACK),
         )
@@ -230,14 +230,13 @@ def tile_picked_tokens_plain_bank_kept_outcomes_endcoarse_kernel(
         for i in range(2):
             nc.scalar.activation(out=m2[i][:].indirect(l6[:]), in_=m1[i][:], func=ACT.Copy)
             put_p(i, 1)
-            for c in range(2):
-                y = tile(f"y{i}{c}", [P, G // 2, 2], F32)
+            cuts = ((0, G), (0, 3 * G // 4, G))[i]
+            for lo, hi in zip(cuts, cuts[1:]):
+                y = tile(f"y{i}_{lo}", [P, hi - lo, 2], F32)
                 nc.vector.tensor_tensor(
                     y[:],
-                    m0[i][:, U // 2 * c : U // 2 * (c + 1)].rearrange("p (g d) -> p g d", d=2),
-                    m2[i][:, G // 2 * c : G // 2 * (c + 1)].unsqueeze(2).to_broadcast([P, G // 2, 2]),
+                    m0[i][:, 2 * lo : 2 * hi].rearrange("p (g d) -> p g d", d=2),
+                    m2[i][:, lo:hi].unsqueeze(2).to_broadcast([P, hi - lo, 2]),
                     ALU.subtract,
                 )
-                (nc.scalar if (i, c) == (1, 1) else nc.sync).dma_start(
-                    out=out[P * i : P * (i + 1), U // 2 * c : U // 2 * (c + 1)], in_=y[:].rearrange("p g d -> p (g d)")
-                )
+                nc.sync.dma_start(out=out[P * i : P * (i + 1), 2 * lo : 2 * hi], in_=y[:].rearrange("p g d -> p (g d)"))

from contextlib import ExitStack

import concourse.mybir as mybir

K, J, R, T, Z, M, O, N, U, E, G = 512, 512, 512, 2048, 512, 1024, 256, 256, 512, 128, 256
FLOPS = 2 * (K * R * J + Z * R * J + 2 * R * N * O)

F32 = mybir.dt.float32
BF16 = mybir.dt.bfloat16
I32 = mybir.dt.int32
U32 = mybir.dt.uint32
U16 = mybir.dt.uint16
U8 = mybir.dt.uint8
FP8X4 = mybir.dt.float8_e4m3fn_x4
FP4X4 = mybir.dt.float4_e2m1fn_x4
ACT = mybir.ActivationFunctionType
ALU = mybir.AluOpType

P = 128
PACK = 4
QUADS = 4
JH = J // 2
OH = O // 2
XT_ROW = 4
W_ROW = 4
WO_ROW = 12


def tile_picked_tokens_plain_bank_kept_outcomes_endcoarse_kernel(
    tc, xt_words, xt_scales, w_words, w_scales, xo_words, xo_scales, w2_words, w2_scales, sa,
    wb_words, wb_scales, wo_words, wo_scales, se, offs, offs2, offs3, offs4, offs5, offs6, out
):
    nc = tc.nc
    with ExitStack() as ctx:
        sb = ctx.enter_context(tc.tile_pool(name="sb", bufs=1))
        ps = ctx.enter_context(tc.psum_pool(name="ps", bufs=1))

        def tile(name, shape, dtype, tag=None):
            return sb.tile(shape, dtype, name=name, tag=tag or name, align_bytes=64)

        def load_list(name, src):
            t = tile(name, list(src.shape), U16)
            nc.sync.dma_start(out=t[:], in_=src)
            return t

        def load_words(eng, name, src, cols):
            t = tile(name, [P, cols], U32)
            eng.dma_start(out=t[:].bitcast(I32), in_=src[0].rearrange("p n t -> p (n t)").bitcast(I32))
            return t

        def load_nibbles(eng, name, src, cols):
            t = tile(name, [P, 2 * cols], U8)
            eng.dma_start(out=t[:].bitcast(I32), in_=src[0].bitcast(I32))
            return t

        def zeroed(name, cols):
            t = tile(name, [P, cols], U8)
            nc.vector.memset(t[:].bitcast(I32), 0)
            return t

        def load_rows(eng, plane, src, row, q):
            eng.dma_start(
                out=plane[32 * q + row : 32 * q + row + 4, :].bitcast(I32),
                in_=src[0, 4 * q : 4 * q + 4, :].bitcast(I32),
            )

        def load_stage(eng, stage, src, row):
            eng.dma_start(
                out=stage[row : row + 4, :].bitcast(I32).rearrange("r (q c) -> r q c", q=QUADS),
                in_=src[0].bitcast(I32).rearrange("(q r) c -> r q c", r=4),
            )

        def spread(plane, stage, cols, quads):
            for q in quads:
                nc.vector.tensor_copy(
                    plane[32 * q : 32 * (q + 1), :cols].bitcast(I32), stage[:32, cols * q : cols * (q + 1)].bitcast(I32)
                )

        xo_s = zeroed("xo_s", M)
        xt_s = zeroed("xt_s", T)
        ww_s = zeroed("ww_s", 2 * R)
        ww_stage = tile("ww_stage", [8, QUADS * R], U8)
        wbo_s = zeroed("wbo_s", QUADS * N)
        floor = tile("floor", [P, 1], F32)
        nc.vector.memset(floor[:], 0.0)
        m0 = [tile(f"m0_{i}", [P, U], F32) for i in range(2)]
        for i in range(2):
            nc.vector.memset(m0[i][:], 0.0)

        w2_w = load_nibbles(nc.gpsimd, "w2_w", w2_words, R)
        load_stage(nc.sync, ww_stage, w2_scales, 0)
        load_stage(nc.sync, ww_stage, w_scales, W_ROW)
        l2 = load_list("l2", offs2)
        for q in range(QUADS):
            load_rows(nc.sync, xo_s, xo_scales, 0, q)
        xo_w = load_words(nc.sync, "xo_w", xo_words, M)
        l1 = load_list("l1", offs)
        for q in range(QUADS):
            load_rows(nc.sync, xt_s, xt_scales, XT_ROW, q)
        xt_w = load_words(nc.sync, "xt_w", xt_words, T)
        w_w = load_words(nc.sync, "w_w", w_words, R)
        l3 = load_list("l3", offs3)
        sa_t = tile("sa_t", [P, PACK], F32)
        nc.sync.dma_start(out=sa_t[:], in_=sa.rearrange("(p t) o -> p (t o)", t=PACK))
        load_stage(nc.sync, wbo_s, wb_scales, 0)
        load_stage(nc.sync, wbo_s, wo_scales, WO_ROW)
        wb_w = load_nibbles(nc.sync, "wb_w", wb_words, N)
        wo_w = load_words(nc.sync, "wo_w", wo_words, N)
        l4 = load_list("l4", offs4)
        l5 = load_list("l5", offs5)
        l6 = load_list("l6", offs6)
        se_t = tile("se_t", [P, 2], F32)
        with nc.allow_non_contiguous_dma(reason="one weight a partition"):
            nc.sync.dma_start(out=se_t[:], in_=se.rearrange("(i p) o -> p (i o)", p=P))

        stage_i = ww_stage[:].bitcast(I32).rearrange("r (a b c) -> r a b c", a=2, b=2)
        plane_i = ww_s[:].bitcast(I32).rearrange("p (a c) -> p a c", a=2)
        nc.vector.tensor_copy(plane_i[0:8], stage_i[:, :, 0, :])
        for a in range(2):
            nc.vector.tensor_copy(plane_i[32:40, a, :], stage_i[:, a, 1, :])
        nc.vector.tensor_copy(plane_i[64:128, 0, :], plane_i[0:64, 1, :])
        ww_sd = tile("ww_sd", [P, R], U8)
        nc.gpsimd.tensor_copy(
            out=ww_sd[:].rearrange("p (t m) -> p t m", t=PACK),
            in_=ww_s[:, :R].rearrange("p (m t) -> p t m", t=PACK),
        )
        xo_sg = tile("xo_sg", [P, J], U8)
        nc.vector.tensor_copy(xo_sg[:], xo_s[:].indirect(l2[:]))

        w2_d = tile("w2_d", [P, 2 * R], U8)
        nc.scalar.copy(
            out=w2_d[:].bitcast(U16).rearrange("p (t c i) -> p c t i", t=PACK, i=8),
            in_=w2_w[:].bitcast(U16).rearrange("p (c i t) -> p c t i", t=PACK, i=8),
        )
        banks = [[ps.tile([P, JH], F32, name=f"a{t}{jh}", tag=f"bank{2 * t + jh}") for jh in range(2)] for t in range(PACK)]
        for jh in range(2):
            xo_wg = tile(f"xo_wg{jh}", [P, JH], U32)
            nc.vector.tensor_copy(xo_wg[:], xo_w[:].indirect(l2[:, JH // 16 * jh : JH // 16 * (jh + 1)]))
            for t in range(PACK):
                nc.tensor.matmul_mx(
                    banks[t][jh][:],
                    lhsT=w2_d[:, 2 * P * t : 2 * P * (t + 1)].bitcast(FP4X4),
                    lhsT_scale=ww_sd[:, P * t : P * (t + 1)],
                    rhs=xo_wg[:].bitcast(FP8X4),
                    rhs_scale=xo_sg[:, JH * jh : JH * (jh + 1)],
                    start=True,
                    stop=False,
                )

        xt_sg = tile("xt_sg", [P, J], U8)
        nc.vector.tensor_copy(xt_sg[:], xt_s[:].indirect(l1[:]))
        w_d = tile("w_d", [P, R], U32)
        for t in range(PACK):
            nc.scalar.copy(out=w_d[:, P * t : P * (t + 1)], in_=w_w[:, t::PACK])
        g1 = [tile(f"g1_{t}", [P, J], F32) for t in range(PACK)]
        for jh in range(2):
            xt_wg = tile(f"xt_wg{jh}", [P, JH], U32)
            nc.vector.tensor_copy(xt_wg[:], xt_w[:].indirect(l1[:, JH // 16 * jh : JH // 16 * (jh + 1)]))
            for t in range(PACK):
                nc.tensor.matmul_mx(
                    banks[t][jh][:],
                    lhsT=w_d[:, P * t : P * (t + 1)].bitcast(FP8X4),
                    lhsT_scale=ww_sd[W_ROW:, P * t : P * (t + 1)],
                    rhs=xt_wg[:].bitcast(FP8X4),
                    rhs_scale=xt_sg[XT_ROW:, JH * jh : JH * (jh + 1)],
                    start=False,
                    stop=True,
                )
        for t in range(PACK - 1):
            nc.scalar.activation(out=g1[t][:, :JH], in_=banks[t][0][:], func=ACT.Relu)
        nc.vector.tensor_scalar_max(g1[PACK - 1][:, :JH], banks[PACK - 1][0][:], floor[:])
        for t in range(PACK):
            nc.vector.tensor_scalar_max(g1[t][:, JH:], banks[t][1][:], floor[:])
        wbo_p = tile("wbo_p", [P, N], U8, tag="floor")
        spread(wbo_p, wbo_s, N, range(QUADS))

        planes = [tile("planes0", [P, PACK, OH], BF16), tile("planes1", [P, PACK, OH], BF16, tag="wbo_s")]
        for h in range(2):
            for t in range(PACK):
                nc.scalar.activation(
                    out=planes[h][:, t, :],
                    in_=g1[t][:].indirect(l3[:, OH // 16 * h : OH // 16 * (h + 1)]),
                    func=ACT.Copy,
                    scale=sa_t[:, t : t + 1],
                )

        p_sb = [[tile(f"p_sb{i}{h}", [P, OH], F32) for h in range(2)] for i in range(2)]
        m2 = []
        q_sb = [tile(f"q_sb{i}", [P, O], F32) for i in range(2)]
        for h in range(2):
            woven = tile("woven", [P, OH, PACK], BF16)
            nc.vector.tensor_copy(
                woven[:].rearrange("p (c i) t -> p c t i", i=4), planes[h][:].rearrange("p t (c i) -> p c t i", i=4)
            )
            m2.append(tile(f"m2_{h}", [P, G], F32, tag=("planes0", "wbo_s")[h]))
            nc.vector.memset(m2[h][:], 0.0)
            codes = tile(f"codes{h}", [P, OH], U32)
            scales = tile(f"scales{h}", [P, OH], U8)
            nc.vector.quantize_mx(codes[:].bitcast(FP8X4), scales[:], woven[:].rearrange("p n t -> p (n t)"))
            for which in ((0, 1) if h == 0 else (1, 0)):
                for i in range(2):
                    acc = ps.tile([P, OH], F32, name=f"acc{h}{which}{i}", tag=f"bank{2 * (2 * which + i) + h}")
                    if which == 0:
                        lhsT = wb_w[:, 2 * P * i : 2 * P * (i + 1)].bitcast(FP4X4)
                        lhsT_scale = wbo_p[:, P * i : P * (i + 1)]
                        dst = p_sb[i][h][:]
                    else:
                        lhsT = wo_w[:, P * i : P * (i + 1)].bitcast(FP8X4)
                        lhsT_scale = wbo_p[WO_ROW:, P * i : P * (i + 1)]
                        dst = q_sb[i][:, OH * h : OH * (h + 1)]
                    nc.tensor.matmul_mx(
                        acc[:], lhsT=lhsT, lhsT_scale=lhsT_scale, rhs=codes[:].bitcast(FP8X4), rhs_scale=scales[:],
                        start=True, stop=True,
                    )
                    if (h, which) == (0, 0):
                        nc.scalar.copy(dst, acc[:])
                    else:
                        nc.vector.tensor_copy(dst, acc[:])

        def put_p(i, h):
            nc.scalar.activation(
                out=m0[i][:].indirect(l4[:, OH // 16 * h : OH // 16 * (h + 1)]), in_=p_sb[i][h][:], func=ACT.Copy
            )

        for i in range(2):
            put_p(i, 0)
        m1 = [tile(f"m1_{i}", [P, E], F32) for i in range(2)]
        for i in range(2):
            nc.scalar.activation(out=m1[i][:], in_=q_sb[i][:].indirect(l5[:]), func=ACT.Copy, scale=se_t[:, i : i + 1])
        for i in range(2):
            nc.scalar.activation(out=m2[i][:].indirect(l6[:]), in_=m1[i][:], func=ACT.Copy)
            put_p(i, 1)
            cuts = ((0, G), (0, 3 * G // 4, G))[i]
            for lo, hi in zip(cuts, cuts[1:]):
                y = tile(f"y{i}_{lo}", [P, hi - lo, 2], F32)
                nc.vector.tensor_tensor(
                    y[:],
                    m0[i][:, 2 * lo : 2 * hi].rearrange("p (g d) -> p g d", d=2),
                    m2[i][:, lo:hi].unsqueeze(2).to_broadcast([P, hi - lo, 2]),
                    ALU.subtract,
                )
                nc.sync.dma_start(out=out[P * i : P * (i + 1), 2 * lo : 2 * hi], in_=y[:].rearrange("p g d -> p (g d)"))
